import numpy as np
import ml_dtypes


def mxq(x, axis, fmt="e4m3"):
    dtype, down = {"e4m3": (ml_dtypes.float8_e4m3fn, 7), "e5m2": (ml_dtypes.float8_e5m2, 14)}[fmt]
    v = np.moveaxis(np.asarray(x, np.float32).astype(ml_dtypes.bfloat16).astype(np.float64), axis, -1)
    blocks = v.reshape(v.shape[:-1] + (-1, 32))
    amax = np.abs(blocks).max(-1, keepdims=True)
    byte = np.maximum(np.where(amax > 0, np.frexp(amax)[1] - 1 + 127, 0) - down, 1)
    scale = np.exp2(byte - 127.0)
    codes = (blocks / scale).astype(np.float32).astype(dtype).astype(np.float64)
    return np.moveaxis((codes * scale).reshape(v.shape), -1, axis)


WIDE = False


def mx_kscale(k):
    if not WIDE:
        return np.ones(k)
    levels = np.array([10, -10, 5, -5, 0])
    if k % 512:
        return np.exp2(np.random.permutation(np.resize(levels, k // 32))).repeat(32)
    a = np.empty((k // 512, 16))
    for p in range(k // 512):
        a[p, :8] = np.random.permutation(np.resize(levels, 8))
        for g in range(8):
            far = levels[np.abs(levels - a[p, g]) >= 10]
            a[p, g + 8] = far[np.random.randint(len(far))]
    return np.exp2(a.ravel()).repeat(32)


def f64(x):
    return np.asarray(x).astype(np.float64)


def striped(idx):
    return np.tile(idx.reshape(-1, 16).T, (8, 1)).astype(np.uint16)


def unstriped(offs):
    return offs[:16].T.reshape(-1).astype(np.int64)


def pack_weight(w):
    k, n = w.shape
    w = f64(np.asarray(w, np.float32).astype(ml_dtypes.bfloat16)).reshape(k // 32, 32, n)
    amax = np.abs(w).max(1)
    byte = np.clip(np.where(amax > 0, np.frexp(amax)[1] - 1 + 127 - 7, 1), 1, 254)
    scaled = (w * np.exp2(127.0 - byte)[:, None, :]).reshape(k, n).astype(np.float32)
    words = np.ascontiguousarray(scaled.reshape(k // 512, 128, 4, n).transpose(0, 1, 3, 2)).astype(ml_dtypes.float8_e4m3fn).view(np.uint8)
    return words, np.ascontiguousarray(byte.astype(np.uint8).reshape(k // 512, 16, n))


def unpack_weight(words, scales):
    g, p, n, _ = words.shape
    vals = np.ascontiguousarray(words).view(ml_dtypes.float8_e4m3fn).astype(np.float64) * np.repeat(np.exp2(scales.astype(np.float64) - 127.0), 8, axis=1)[..., None]
    return vals.transpose(0, 1, 3, 2).reshape(g * 512, n)


def relu(v):
    return np.maximum(v, 0.0)


K, T, S, V = 1024, 2048, 512, 512
P = 2 ** 7


def setup_inputs():
    n = np.random.standard_normal
    s = mx_kscale(K)[:, None]
    packed_xT = pack_weight(n((K, T)) * s)
    return {
        "x_words": packed_xT[0],
        "x_scales": packed_xT[1],
        "hT": (n((K, V)) / np.sqrt(K) / s).astype(np.float32),
        "rad": (np.tile(np.random.uniform(0.8, 1.6, T), (P, 1))).astype(np.float32),
        "rf": (np.tile(np.random.uniform(1.1, 1.6, T), (P, 1))).astype(np.float32),
        "qn": (np.random.uniform(0.8, 1.6, (V, 1))).astype(np.float32),
        "offs": striped(np.random.permutation(T)[:S]),
    }


def reference(x_words, x_scales, hT, rad, rf, qn, offs):
    hTq = mxq(f64(hT), 0, "e4m3")
    xq = unpack_weight(x_words, x_scales)[:, unstriped(offs)]
    y = hTq.T @ xq
    ip = f64(qn) * ((0.3 * (y * (f64(rad)[:1][:, unstriped(offs)]))) * (f64(rf)[:1][:, unstriped(offs)]))
    ds = (f64(rad)[:1][:, unstriped(offs)]) ** 2 - (2.0 * ip)
    er = f64(qn) * (0.3 * ((f64(rad)[:1][:, unstriped(offs)]) * (np.sqrt((f64(rf)[:1][:, unstriped(offs)]) ** 2 - 1.0))))
    ub = ds + er
    best = ub.min(axis=1, keepdims=True)
    return relu(-1.0 * (ds - er - best))

@@ -1,0 +1,234 @@
+from contextlib import ExitStack
+
+import concourse.mybir as mybir
+
+K, T, S, V = 1024, 2048, 512, 512
+FLOPS = 2 * K * S * V
+BYTES = K * T + K * T // 32 + 4 * K * V + 2 * 4 * T + 4 * V + 2 * 128 * 32 + 4 * V * S
+
+F32 = mybir.dt.float32
+BF16 = mybir.dt.bfloat16
+I32 = mybir.dt.int32
+U32 = mybir.dt.uint32
+U16 = mybir.dt.uint16
+U8 = mybir.dt.uint8
+FP8X4 = mybir.dt.float8_e4m3fn_x4
+ALU = mybir.AluOpType
+ACT = mybir.ActivationFunctionType
+
+P = 128
+PACK = 4
+PASSES = 2
+TILES = 4
+HALF = 256
+
+
+def tile_picked_yrabit_gap_p_kernel(
+    tc, x_words, x_scales, hT, rad, rf, qn, offs, out
+):
+    nc = tc.nc
+    with ExitStack() as ctx:
+        sb = ctx.enter_context(tc.tile_pool(name="sb", bufs=1))
+        ps = ctx.enter_context(tc.psum_pool(name="ps", bufs=1))
+
+        offsets = sb.tile([P, S // 16], U16, name="offsets")
+        nc.sync.dma_start(offsets[:], offs)
+
+        def load_queries(g):
+            raw = sb.tile([P, PACK, V], F32, name=f"h_raw{g}", tag=f"h_raw{g}")
+            nc.sync.dma_start(
+                raw[:], hT[512 * g : 512 * (g + 1), :].rearrange("(p j) t -> p j t", j=PACK)
+            )
+            return raw
+
+        h_raw = [load_queries(0)]
+
+        q_col = sb.tile([P, TILES], F32, name="q_col", tag="mid", align_bytes=64)
+        nc.scalar.dma_start(q_col[:], qn.rearrange("(p c) o -> p (c o)", c=TILES))
+
+        warm = sb.tile([P, 1], F32, name="warm")
+        nc.gpsimd.memset(warm[:], 1.0)
+        warmed = sb.tile([P, 1], F32, name="warmed")
+        nc.scalar.activation(warmed[:], warm[:], ACT.Sqrt)
+
+        side_tab = sb.tile([P, T], F32, name="side_tab")
+        nc.vector.memset(side_tab[:], 0.0)
+        nc.scalar.dma_start(side_tab[0:1, :], rad[0:1, :])
+        nc.scalar.dma_start(side_tab[1:2, :], rf[0:1, :])
+
+        s_tab = sb.tile([P, T], U8, name="s_tab", align_bytes=64)
+        nc.gpsimd.memset(s_tab[:].bitcast(I32), 0)
+        for quad in range(4):
+            nc.scalar.dma_start(
+                s_tab[32 * quad : 32 * quad + 8, :].bitcast(I32),
+                x_scales[:, 4 * quad : 4 * quad + 4, :].bitcast(I32),
+            )
+
+        zeros = sb.tile([P, P], F32, name="zeros", tag="h_raw1")
+        nc.vector.memset(zeros[:], 0.0)
+        ident = sb.tile([P, P], F32, name="ident")
+        nc.gpsimd.affine_select(
+            out=ident[:], in_=zeros[:], pattern=[[-1, P]], compare_op=ALU.not_equal,
+            fill=1.0, base=0, channel_multiplier=1,
+        )
+        h_raw.append(load_queries(1))
+
+        q_bank = ps.tile([P, TILES, P], F32, name="q_bank", tag="y2")
+        for c in range(TILES):
+            nc.tensor.transpose(
+                q_bank[:, c, :], q_col[:, c : c + 1].to_broadcast([P, P]), ident[:]
+            )
+        x_all = sb.tile([P, PASSES * T], U32, name="x_all", tag="mid", align_bytes=64)
+        x_tab = [x_all[:, g * T : (g + 1) * T] for g in range(PASSES)]
+        for g in range(PASSES):
+            nc.sync.dma_start(
+                x_tab[g].bitcast(I32), x_words[g].rearrange("p c r -> p (c r)").bitcast(I32)
+            )
+        q_row = sb.tile([P, V], F32, name="q_row")
+        nc.scalar.copy(
+            q_row[:].rearrange("x (p c) -> x p c", c=TILES),
+            q_bank[:].rearrange("x c p -> x p c"),
+        )
+
+        side = sb.tile([P, S], F32, name="side")
+        nc.vector.tensor_copy(side[:], side_tab[:].indirect(offsets[:]))
+        side_bank = ps.tile([P, TILES, P], F32, name="side_bank", tag="y3")
+        for jt in range(TILES):
+            nc.tensor.transpose(side_bank[:, jt, :], side[:, jt * P : (jt + 1) * P], ident[:])
+        side_col = sb.tile([P, TILES, 2], F32, name="side_col")
+        nc.scalar.copy(side_col[:], side_bank[:, :, 0:2])
+        squares = sb.tile([P, TILES, 2], F32, name="squares")
+        nc.scalar.activation(squares[:], side_bank[:, :, 0:2], ACT.Square)
+        root = sb.tile([P, TILES], F32, name="root")
+        nc.scalar.activation(root[:], squares[:, :, 1], ACT.Sqrt, bias=-1.0)
+        slope = sb.tile([P, TILES], F32, name="slope")
+        nc.vector.scalar_tensor_tensor(
+            slope[:], side_col[:, :, 0], 0.6, side_col[:, :, 1], ALU.mult, ALU.mult
+        )
+        neg_r2 = sb.tile([P, TILES], F32, name="neg_r2")
+        nc.vector.tensor_scalar(neg_r2[:], squares[:, :, 0], -1.0, None, ALU.mult)
+        neg_err = sb.tile([P, TILES], F32, name="neg_err")
+        nc.vector.scalar_tensor_tensor(
+            neg_err[:], root[:], -0.3, side_col[:, :, 0], ALU.mult, ALU.mult
+        )
+        two_err = sb.tile([P, TILES], F32, name="two_err")
+        nc.vector.scalar_tensor_tensor(
+            two_err[:], root[:], 0.6, side_col[:, :, 0], ALU.mult, ALU.mult
+        )
+
+        h_codes, h_scales = [], []
+        for g in range(PASSES):
+            codes = sb.tile([P, V], U32, name=f"h_codes{g}", align_bytes=64)
+            scales = sb.tile([P, V], U8, name=f"h_scales{g}", align_bytes=64)
+            grouped = []
+            for half in range(2):
+                cols = slice(half * HALF, (half + 1) * HALF)
+                grp = sb.tile([P, HALF, PACK], BF16, name=f"h_grp{g}{half}", align_bytes=64)
+                dst = grp[:].rearrange("p (c i) j -> p c j i", i=4)
+                srcv = h_raw[g][:, :, cols].rearrange("p j (c i) -> p c j i", i=4)
+                if half == 0:
+                    nc.vector.tensor_copy(dst, srcv)
+                else:
+                    nc.scalar.copy(dst, srcv)
+                grouped.append(grp)
+            for half in range(2):
+                cols = slice(half * HALF, (half + 1) * HALF)
+                nc.vector.quantize_mx(
+                    out=codes[:, cols].bitcast(FP8X4),
+                    scales=scales[:, cols],
+                    in_=grouped[half][:].rearrange("p c j -> p (c j)"),
+                )
+            h_codes.append(codes)
+            h_scales.append(scales)
+
+        low = [ps.tile([P, S], F32, name=f"low{tt}", tag=f"low{tt}") for tt in range(TILES)]
+        for jt in range(TILES):
+            base = sb.tile([P, V], F32, name=f"base{jt}")
+            nc.scalar.activation(
+                base[:], q_row[:], ACT.Identity,
+                bias=neg_r2[:, jt : jt + 1], scale=two_err[:, jt : jt + 1],
+            )
+            for tt in range(TILES):
+                nc.tensor.matmul(
+                    low[tt][:, jt * P : (jt + 1) * P], base[:, tt * P : (tt + 1) * P], ident[:],
+                    start=(jt == 0), stop=False, is_transpose=True,
+                )
+
+        x_sc = sb.tile([P, S], U8, name="x_sc", align_bytes=64)
+        nc.vector.tensor_copy(x_sc[:], s_tab[:].indirect(offsets[:]))
+        x_codes = {}
+        first = sb.tile([P, S], U32, name="x_codes0", align_bytes=64)
+        nc.vector.tensor_copy(first[:], x_tab[0].indirect(offsets[:]))
+        for jt in range(TILES):
+            x_codes[(0, jt)] = first[:, jt * P : (jt + 1) * P]
+        for half in range(2):
+            part = sb.tile([P, HALF], U32, name=f"x_codes1{half}", align_bytes=64)
+            nc.vector.tensor_copy(
+                part[:], x_tab[1].indirect(offsets[:, half * 16 : (half + 1) * 16])
+            )
+            for i in range(2):
+                x_codes[(1, 2 * half + i)] = part[:, i * P : (i + 1) * P]
+
+        prod = [ps.tile([P, V], F32, name=f"prod{jt}", tag=f"y{jt}") for jt in range(TILES)]
+        for g in range(PASSES):
+            for jt in range(TILES):
+                nc.tensor.matmul_mx(
+                    out=prod[jt][:],
+                    lhsT=x_codes[(g, jt)].bitcast(FP8X4),
+                    lhsT_scale=x_sc[4 * g : P, jt * P : (jt + 1) * P],
+                    rhs=h_codes[g][:].bitcast(FP8X4),
+                    rhs_scale=h_scales[g][:],
+                    start=(g == 0),
+                    stop=(g == PASSES - 1),
+                )
+
+        fit = {}
+        for half in range(2):
+            cols = slice(half * HALF, (half + 1) * HALF)
+            for jt in range(TILES):
+                tile_fit = sb.tile([P, HALF], F32, name=f"fit{half}{jt}")
+                nc.scalar.activation(
+                    tile_fit[:], prod[jt][:, cols], ACT.Identity,
+                    bias=neg_err[:, jt : jt + 1], scale=slope[:, jt : jt + 1],
+                )
+                fit[(half, jt)] = tile_fit
+
+        for half in range(2):
+            cols = slice(half * HALF, (half + 1) * HALF)
+            term = []
+            for jt in range(TILES):
+                tile_term = sb.tile([P, HALF], F32, name=f"term{half}{jt}")
+                nc.vector.tensor_tensor(tile_term[:], fit[(half, jt)][:], q_row[:, cols], ALU.mult)
+                term.append(tile_term)
+                for i in range(2):
+                    nc.tensor.matmul(
+                        low[2 * half + i][:, jt * P : (jt + 1) * P],
+                        tile_term[:, i * P : (i + 1) * P], ident[:],
+                        start=False, stop=(jt == TILES - 1), is_transpose=True,
+                    )
+            top = sb.tile([P, HALF], F32, name=f"top{half}0")
+            nc.vector.tensor_scalar(top[:], term[0][:], neg_r2[:, 0:1], None, ALU.add)
+            for jt in range(1, TILES):
+                nxt = sb.tile([P, HALF], F32, name=f"top{half}{jt}")
+                nc.vector.scalar_tensor_tensor(
+                    nxt[:], term[jt][:], neg_r2[:, jt : jt + 1], top[:], ALU.add, ALU.max
+                )
+                top = nxt
+            top_bank = ps.tile([P, 2, P], F32, name=f"top_bank{half}", tag=f"y{half}")
+            for i in range(2):
+                nc.tensor.transpose(top_bank[:, i, :], top[:, i * P : (i + 1) * P], ident[:])
+            for i in range(2):
+                tt = 2 * half + i
+                spare = sb.tile([P, P], F32, name=f"upper{tt}")
+                best = sb.tile([P, 1], F32, name=f"best{tt}")
+                nc.vector.tensor_scalar(
+                    spare[:], top_bank[:, i, :], -1.0, None, ALU.mult, ALU.min, accum_out=best[:]
+                )
+                res = sb.tile([P, S], F32, name=f"res{tt}")
+                if tt == TILES - 1:
+                    nc.vector.tensor_scalar(
+                        res[:], low[tt][:], best[:, 0:1], 0.0, ALU.add, ALU.max
+                    )
+                else:
+                    nc.scalar.activation(res[:], low[tt][:], ACT.Relu, bias=best[:, 0:1])
+                nc.sync.dma_start(out[tt * P : (tt + 1) * P, :], res[:])

@@ -15,6 +15,7 @@ U8 = mybir.dt.uint8
 FP8X4 = mybir.dt.float8_e4m3fn_x4
 ALU = mybir.AluOpType
 ACT = mybir.ActivationFunctionType
+AXIS = mybir.AxisListType
 
 P = 128
 PACK = 4
@@ -34,14 +35,21 @@ def tile_picked_yrabit_gap_p_kernel(
         offsets = sb.tile([P, S // 16], U16, name="offsets")
         nc.sync.dma_start(offsets[:], offs)
 
-        def load_queries(g):
-            raw = sb.tile([P, PACK, V], F32, name=f"h_raw{g}", tag=f"h_raw{g}")
+        def load_queries(g, tag):
+            raw = sb.tile([P, PACK, V], F32, name=f"h_raw{g}", tag=tag, align_bytes=64)
             nc.sync.dma_start(
                 raw[:], hT[512 * g : 512 * (g + 1), :].rearrange("(p j) t -> p j t", j=PACK)
             )
             return raw
 
-        h_raw = [load_queries(0)]
+        def load_words(g, tag):
+            tab = sb.tile([P, T], U32, name=f"x_tab{g}", tag=tag, align_bytes=64)
+            nc.sync.dma_start(
+                tab[:].bitcast(I32), x_words[g].rearrange("p c r -> p (c r)").bitcast(I32)
+            )
+            return tab
+
+        h_raw = [load_queries(0, "first")]
 
         q_col = sb.tile([P, TILES], F32, name="q_col", tag="mid", align_bytes=64)
         nc.scalar.dma_start(q_col[:], qn.rearrange("(p c) o -> p (c o)", c=TILES))
@@ -51,7 +59,7 @@ def tile_picked_yrabit_gap_p_kernel(
         warmed = sb.tile([P, 1], F32, name="warmed")
         nc.scalar.activation(warmed[:], warm[:], ACT.Sqrt)
 
-        side_tab = sb.tile([P, T], F32, name="side_tab")
+        side_tab = sb.tile([P, T], F32, name="side_tab", tag="late", align_bytes=64)
         nc.vector.memset(side_tab[:], 0.0)
         nc.scalar.dma_start(side_tab[0:1, :], rad[0:1, :])
         nc.scalar.dma_start(side_tab[1:2, :], rf[0:1, :])
@@ -64,26 +72,21 @@ def tile_picked_yrabit_gap_p_kernel(
                 x_scales[:, 4 * quad : 4 * quad + 4, :].bitcast(I32),
             )
 
-        zeros = sb.tile([P, P], F32, name="zeros", tag="h_raw1")
+        zeros = sb.tile([P, P], F32, name="zeros", tag="second", align_bytes=64)
         nc.vector.memset(zeros[:], 0.0)
         ident = sb.tile([P, P], F32, name="ident")
         nc.gpsimd.affine_select(
             out=ident[:], in_=zeros[:], pattern=[[-1, P]], compare_op=ALU.not_equal,
             fill=1.0, base=0, channel_multiplier=1,
         )
-        h_raw.append(load_queries(1))
+        x_tab = [load_words(0, "second")]
 
         q_bank = ps.tile([P, TILES, P], F32, name="q_bank", tag="y2")
         for c in range(TILES):
             nc.tensor.transpose(
                 q_bank[:, c, :], q_col[:, c : c + 1].to_broadcast([P, P]), ident[:]
             )
-        x_all = sb.tile([P, PASSES * T], U32, name="x_all", tag="mid", align_bytes=64)
-        x_tab = [x_all[:, g * T : (g + 1) * T] for g in range(PASSES)]
-        for g in range(PASSES):
-            nc.sync.dma_start(
-                x_tab[g].bitcast(I32), x_words[g].rearrange("p c r -> p (c r)").bitcast(I32)
-            )
+        h_raw.append(load_queries(1, "mid"))
         q_row = sb.tile([P, V], F32, name="q_row")
         nc.scalar.copy(
             q_row[:].rearrange("x (p c) -> x p c", c=TILES),
@@ -92,6 +95,7 @@ def tile_picked_yrabit_gap_p_kernel(
 
         side = sb.tile([P, S], F32, name="side")
         nc.vector.tensor_copy(side[:], side_tab[:].indirect(offsets[:]))
+        x_tab.append(load_words(1, "late"))
         side_bank = ps.tile([P, TILES, P], F32, name="side_bank", tag="y3")
         for jt in range(TILES):
             nc.tensor.transpose(side_bank[:, jt, :], side[:, jt * P : (jt + 1) * P], ident[:])
@@ -107,6 +111,10 @@ def tile_picked_yrabit_gap_p_kernel(
         )
         neg_r2 = sb.tile([P, TILES], F32, name="neg_r2")
         nc.vector.tensor_scalar(neg_r2[:], squares[:, :, 0], -1.0, None, ALU.mult)
+        shift = sb.tile([P, TILES], F32, name="shift")
+        nc.vector.tensor_scalar(
+            shift[:], squares[:, :, 0], squares[:, 0, 0:1], -1.0, ALU.subtract, ALU.mult
+        )
         neg_err = sb.tile([P, TILES], F32, name="neg_err")
         nc.vector.scalar_tensor_tensor(
             neg_err[:], root[:], -0.3, side_col[:, :, 0], ALU.mult, ALU.mult
@@ -115,6 +123,14 @@ def tile_picked_yrabit_gap_p_kernel(
         nc.vector.scalar_tensor_tensor(
             two_err[:], root[:], 0.6, side_col[:, :, 0], ALU.mult, ALU.mult
         )
+
+        x_sc = sb.tile([P, S], U8, name="x_sc", align_bytes=64)
+        nc.vector.tensor_copy(x_sc[:], s_tab[:].indirect(offsets[:]))
+        x_codes = {}
+        first = sb.tile([P, S], U32, name="x_codes0", align_bytes=64)
+        nc.vector.tensor_copy(first[:], x_tab[0][:].indirect(offsets[:]))
+        for jt in range(TILES):
+            x_codes[(0, jt)] = first[:, jt * P : (jt + 1) * P]
 
         h_codes, h_scales = [], []
         for g in range(PASSES):
@@ -126,7 +142,7 @@ def tile_picked_yrabit_gap_p_kernel(
                 grp = sb.tile([P, HALF, PACK], BF16, name=f"h_grp{g}{half}", align_bytes=64)
                 dst = grp[:].rearrange("p (c i) j -> p c j i", i=4)
                 srcv = h_raw[g][:, :, cols].rearrange("p j (c i) -> p c j i", i=4)
-                if half == 0:
+                if g == 1:
                     nc.vector.tensor_copy(dst, srcv)
                 else:
                     nc.scalar.copy(dst, srcv)
@@ -141,36 +157,9 @@ def tile_picked_yrabit_gap_p_kernel(
             h_codes.append(codes)
             h_scales.append(scales)
 
-        low = [ps.tile([P, S], F32, name=f"low{tt}", tag=f"low{tt}") for tt in range(TILES)]
-        for jt in range(TILES):
-            base = sb.tile([P, V], F32, name=f"base{jt}")
-            nc.scalar.activation(
-                base[:], q_row[:], ACT.Identity,
-                bias=neg_r2[:, jt : jt + 1], scale=two_err[:, jt : jt + 1],
-            )
-            for tt in range(TILES):
-                nc.tensor.matmul(
-                    low[tt][:, jt * P : (jt + 1) * P], base[:, tt * P : (tt + 1) * P], ident[:],
-                    start=(jt == 0), stop=False, is_transpose=True,
-                )
-
-        x_sc = sb.tile([P, S], U8, name="x_sc", align_bytes=64)
-        nc.vector.tensor_copy(x_sc[:], s_tab[:].indirect(offsets[:]))
-        x_codes = {}
-        first = sb.tile([P, S], U32, name="x_codes0", align_bytes=64)
-        nc.vector.tensor_copy(first[:], x_tab[0].indirect(offsets[:]))
-        for jt in range(TILES):
-            x_codes[(0, jt)] = first[:, jt * P : (jt + 1) * P]
-        for half in range(2):
-            part = sb.tile([P, HALF], U32, name=f"x_codes1{half}", align_bytes=64)
-            nc.vector.tensor_copy(
-                part[:], x_tab[1].indirect(offsets[:, half * 16 : (half + 1) * 16])
-            )
-            for i in range(2):
-                x_codes[(1, 2 * half + i)] = part[:, i * P : (i + 1) * P]
-
         prod = [ps.tile([P, V], F32, name=f"prod{jt}", tag=f"y{jt}") for jt in range(TILES)]
-        for g in range(PASSES):
+
+        def multiply(g):
             for jt in range(TILES):
                 nc.tensor.matmul_mx(
                     out=prod[jt][:],
@@ -182,53 +171,97 @@ def tile_picked_yrabit_gap_p_kernel(
                     stop=(g == PASSES - 1),
                 )
 
-        fit = {}
+        multiply(0)
+
+        low = [ps.tile([P, S], F32, name=f"low{tt}", tag=f"low{tt}") for tt in range(TILES)]
+        base = {}
         for half in range(2):
-            cols = slice(half * HALF, (half + 1) * HALF)
             for jt in range(TILES):
-                tile_fit = sb.tile([P, HALF], F32, name=f"fit{half}{jt}")
+                base[(half, jt)] = sb.tile([P, HALF], F32, name=f"base{half}{jt}")
                 nc.scalar.activation(
-                    tile_fit[:], prod[jt][:, cols], ACT.Identity,
-                    bias=neg_err[:, jt : jt + 1], scale=slope[:, jt : jt + 1],
+                    base[(half, jt)][:], q_row[:, half * HALF : (half + 1) * HALF], ACT.Identity,
+                    bias=neg_r2[:, jt : jt + 1], scale=two_err[:, jt : jt + 1],
                 )
-                fit[(half, jt)] = tile_fit
+
+        def add_into_low(half, jt, values, start, stop):
+            for i in range(2):
+                nc.tensor.matmul(
+                    low[2 * half + i][:, jt * P : (jt + 1) * P],
+                    values[:, i * P : (i + 1) * P], ident[:],
+                    start=start, stop=stop, is_transpose=True,
+                )
+
+        for jt in range(TILES):
+            add_into_low(0, jt, base[(0, jt)], jt == 0, False)
 
         for half in range(2):
-            cols = slice(half * HALF, (half + 1) * HALF)
-            term = []
-            for jt in range(TILES):
-                tile_term = sb.tile([P, HALF], F32, name=f"term{half}{jt}")
-                nc.vector.tensor_tensor(tile_term[:], fit[(half, jt)][:], q_row[:, cols], ALU.mult)
-                term.append(tile_term)
-                for i in range(2):
-                    nc.tensor.matmul(
-                        low[2 * half + i][:, jt * P : (jt + 1) * P],
-                        tile_term[:, i * P : (i + 1) * P], ident[:],
-                        start=False, stop=(jt == TILES - 1), is_transpose=True,
-                    )
-            top = sb.tile([P, HALF], F32, name=f"top{half}0")
-            nc.vector.tensor_scalar(top[:], term[0][:], neg_r2[:, 0:1], None, ALU.add)
-            for jt in range(1, TILES):
-                nxt = sb.tile([P, HALF], F32, name=f"top{half}{jt}")
-                nc.vector.scalar_tensor_tensor(
-                    nxt[:], term[jt][:], neg_r2[:, jt : jt + 1], top[:], ALU.add, ALU.max
-                )
-                top = nxt
+            part = sb.tile([P, HALF], U32, name=f"x_codes1{half}", align_bytes=64)
+            nc.vector.tensor_copy(
+                part[:], x_tab[1][:].indirect(offsets[:, half * 16 : (half + 1) * 16])
+            )
+            for i in range(2):
+                x_codes[(1, 2 * half + i)] = part[:, i * P : (i + 1) * P]
+
+        multiply(1)
+
+        steps = [(0, 0), (1, 0), (0, 1), (0, 2), (0, 3), (1, 1), (1, 2), (1, 3)]
+        top = {}
+
+        def finish(half):
             top_bank = ps.tile([P, 2, P], F32, name=f"top_bank{half}", tag=f"y{half}")
             for i in range(2):
-                nc.tensor.transpose(top_bank[:, i, :], top[:, i * P : (i + 1) * P], ident[:])
+                nc.tensor.matmul(
+                    top_bank[:, i, :], neg_r2[:, 0:1].to_broadcast([P, P]), ident[:],
+                    start=(i == 0), stop=False, is_transpose=True,
+                )
+            for i in range(2):
+                nc.tensor.matmul(
+                    top_bank[:, i, :], top[half][:, i * P : (i + 1) * P], ident[:],
+                    start=False, stop=(i == 1), is_transpose=True,
+                )
+            best = sb.tile([P, 2], F32, name=f"best{half}")
+            nc.vector.tensor_reduce(best[:], top_bank[:], AXIS.X, ALU.max, negate=True)
             for i in range(2):
                 tt = 2 * half + i
-                spare = sb.tile([P, P], F32, name=f"upper{tt}")
-                best = sb.tile([P, 1], F32, name=f"best{tt}")
-                nc.vector.tensor_scalar(
-                    spare[:], top_bank[:, i, :], -1.0, None, ALU.mult, ALU.min, accum_out=best[:]
-                )
                 res = sb.tile([P, S], F32, name=f"res{tt}")
                 if tt == TILES - 1:
                     nc.vector.tensor_scalar(
-                        res[:], low[tt][:], best[:, 0:1], 0.0, ALU.add, ALU.max
+                        res[:], low[tt][:], best[:, i : i + 1], 0.0, ALU.add, ALU.max
                     )
                 else:
-                    nc.scalar.activation(res[:], low[tt][:], ACT.Relu, bias=best[:, 0:1])
+                    nc.scalar.activation(res[:], low[tt][:], ACT.Relu, bias=best[:, i : i + 1])
                 nc.sync.dma_start(out[tt * P : (tt + 1) * P, :], res[:])
+
+        def make_term(half, jt):
+            cols = slice(half * HALF, (half + 1) * HALF)
+            fit = sb.tile([P, HALF], F32, name=f"fit{half}{jt}")
+            nc.scalar.activation(
+                fit[:], prod[jt][:, cols], ACT.Identity,
+                bias=neg_err[:, jt : jt + 1], scale=slope[:, jt : jt + 1],
+            )
+            term = sb.tile([P, HALF], F32, name=f"term{half}{jt}")
+            nc.vector.tensor_tensor(term[:], fit[:], q_row[:, cols], ALU.mult)
+            add_into_low(half, jt, term, (half, jt) == (1, 0), jt == TILES - 1)
+            if (half, jt) == (1, 0):
+                for other in range(TILES):
+                    add_into_low(1, other, base[(1, other)], False, False)
+            return term
+
+        def take_maximum(half, jt, term):
+            if jt == 0:
+                top[half] = term
+            else:
+                nxt = sb.tile([P, HALF], F32, name=f"top{half}{jt}")
+                nc.vector.scalar_tensor_tensor(
+                    nxt[:], term[:], shift[:, jt : jt + 1], top[half][:], ALU.add, ALU.max
+                )
+                top[half] = nxt
+            if jt == TILES - 1:
+                finish(half)
+
+        terms = []
+        for n, (half, jt) in enumerate(steps):
+            terms.append(make_term(half, jt))
+            if n > 0:
+                take_maximum(*steps[n - 1], terms[n - 1])
+        take_maximum(*steps[-1], terms[-1])

from contextlib import ExitStack

import concourse.mybir as mybir

K, T, S, V = 1024, 2048, 512, 512
FLOPS = 2 * K * S * V
BYTES = K * T + K * T // 32 + 4 * K * V + 2 * 4 * T + 4 * V + 2 * 128 * 32 + 4 * V * S

F32 = mybir.dt.float32
BF16 = mybir.dt.bfloat16
I32 = mybir.dt.int32
U32 = mybir.dt.uint32
U16 = mybir.dt.uint16
U8 = mybir.dt.uint8
FP8X4 = mybir.dt.float8_e4m3fn_x4
ALU = mybir.AluOpType
ACT = mybir.ActivationFunctionType
AXIS = mybir.AxisListType

P = 128
PACK = 4
PASSES = 2
TILES = 4
HALF = 256


def tile_picked_yrabit_gap_p_kernel(
    tc, x_words, x_scales, hT, rad, rf, qn, offs, out
):
    nc = tc.nc
    with ExitStack() as ctx:
        sb = ctx.enter_context(tc.tile_pool(name="sb", bufs=1))
        ps = ctx.enter_context(tc.psum_pool(name="ps", bufs=1))

        offsets = sb.tile([P, S // 16], U16, name="offsets")
        nc.sync.dma_start(offsets[:], offs)

        def load_queries(g, tag):
            raw = sb.tile([P, PACK, V], F32, name=f"h_raw{g}", tag=tag, align_bytes=64)
            nc.sync.dma_start(
                raw[:], hT[512 * g : 512 * (g + 1), :].rearrange("(p j) t -> p j t", j=PACK)
            )
            return raw

        def load_words(g, tag):
            tab = sb.tile([P, T], U32, name=f"x_tab{g}", tag=tag, align_bytes=64)
            nc.sync.dma_start(
                tab[:].bitcast(I32), x_words[g].rearrange("p c r -> p (c r)").bitcast(I32)
            )
            return tab

        h_raw = [load_queries(0, "first")]

        q_col = sb.tile([P, TILES], F32, name="q_col", tag="mid", align_bytes=64)
        nc.scalar.dma_start(q_col[:], qn.rearrange("(p c) o -> p (c o)", c=TILES))

        warm = sb.tile([P, 1], F32, name="warm")
        nc.gpsimd.memset(warm[:], 1.0)
        warmed = sb.tile([P, 1], F32, name="warmed")
        nc.scalar.activation(warmed[:], warm[:], ACT.Sqrt)

        side_tab = sb.tile([P, T], F32, name="side_tab", tag="late", align_bytes=64)
        nc.vector.memset(side_tab[:], 0.0)
        nc.scalar.dma_start(side_tab[0:1, :], rad[0:1, :])
        nc.scalar.dma_start(side_tab[1:2, :], rf[0:1, :])

        s_tab = sb.tile([P, T], U8, name="s_tab", align_bytes=64)
        nc.gpsimd.memset(s_tab[:].bitcast(I32), 0)
        for quad in range(4):
            nc.scalar.dma_start(
                s_tab[32 * quad : 32 * quad + 8, :].bitcast(I32),
                x_scales[:, 4 * quad : 4 * quad + 4, :].bitcast(I32),
            )

        zeros = sb.tile([P, P], F32, name="zeros", tag="second", align_bytes=64)
        nc.vector.memset(zeros[:], 0.0)
        ident = sb.tile([P, P], F32, name="ident")
        nc.gpsimd.affine_select(
            out=ident[:], in_=zeros[:], pattern=[[-1, P]], compare_op=ALU.not_equal,
            fill=1.0, base=0, channel_multiplier=1,
        )
        x_tab = [load_words(0, "second")]

        q_bank = ps.tile([P, TILES, P], F32, name="q_bank", tag="y2")
        for c in range(TILES):
            nc.tensor.transpose(
                q_bank[:, c, :], q_col[:, c : c + 1].to_broadcast([P, P]), ident[:]
            )
        h_raw.append(load_queries(1, "mid"))
        q_row = sb.tile([P, V], F32, name="q_row")
        nc.scalar.copy(
            q_row[:].rearrange("x (p c) -> x p c", c=TILES),
            q_bank[:].rearrange("x c p -> x p c"),
        )

        side = sb.tile([P, S], F32, name="side")
        nc.vector.tensor_copy(side[:], side_tab[:].indirect(offsets[:]))
        x_tab.append(load_words(1, "late"))
        side_bank = ps.tile([P, TILES, P], F32, name="side_bank", tag="y3")
        for jt in range(TILES):
            nc.tensor.transpose(side_bank[:, jt, :], side[:, jt * P : (jt + 1) * P], ident[:])
        side_col = sb.tile([P, TILES, 2], F32, name="side_col")
        nc.scalar.copy(side_col[:], side_bank[:, :, 0:2])
        squares = sb.tile([P, TILES, 2], F32, name="squares")
        nc.scalar.activation(squares[:], side_bank[:, :, 0:2], ACT.Square)
        root = sb.tile([P, TILES], F32, name="root")
        nc.scalar.activation(root[:], squares[:, :, 1], ACT.Sqrt, bias=-1.0)
        slope = sb.tile([P, TILES], F32, name="slope")
        nc.vector.scalar_tensor_tensor(
            slope[:], side_col[:, :, 0], 0.6, side_col[:, :, 1], ALU.mult, ALU.mult
        )
        neg_r2 = sb.tile([P, TILES], F32, name="neg_r2")
        nc.vector.tensor_scalar(neg_r2[:], squares[:, :, 0], -1.0, None, ALU.mult)
        shift = sb.tile([P, TILES], F32, name="shift")
        nc.vector.tensor_scalar(
            shift[:], squares[:, :, 0], squares[:, 0, 0:1], -1.0, ALU.subtract, ALU.mult
        )
        neg_err = sb.tile([P, TILES], F32, name="neg_err")
        nc.vector.scalar_tensor_tensor(
            neg_err[:], root[:], -0.3, side_col[:, :, 0], ALU.mult, ALU.mult
        )
        two_err = sb.tile([P, TILES], F32, name="two_err")
        nc.vector.scalar_tensor_tensor(
            two_err[:], root[:], 0.6, side_col[:, :, 0], ALU.mult, ALU.mult
        )

        x_sc = sb.tile([P, S], U8, name="x_sc", align_bytes=64)
        nc.vector.tensor_copy(x_sc[:], s_tab[:].indirect(offsets[:]))
        x_codes = {}
        first = sb.tile([P, S], U32, name="x_codes0", align_bytes=64)
        nc.vector.tensor_copy(first[:], x_tab[0][:].indirect(offsets[:]))
        for jt in range(TILES):
            x_codes[(0, jt)] = first[:, jt * P : (jt + 1) * P]

        h_codes, h_scales = [], []
        for g in range(PASSES):
            codes = sb.tile([P, V], U32, name=f"h_codes{g}", align_bytes=64)
            scales = sb.tile([P, V], U8, name=f"h_scales{g}", align_bytes=64)
            grouped = []
            for half in range(2):
                cols = slice(half * HALF, (half + 1) * HALF)
                grp = sb.tile([P, HALF, PACK], BF16, name=f"h_grp{g}{half}", align_bytes=64)
                dst = grp[:].rearrange("p (c i) j -> p c j i", i=4)
                srcv = h_raw[g][:, :, cols].rearrange("p j (c i) -> p c j i", i=4)
                if g == 1:
                    nc.vector.tensor_copy(dst, srcv)
                else:
                    nc.scalar.copy(dst, srcv)
                grouped.append(grp)
            for half in range(2):
                cols = slice(half * HALF, (half + 1) * HALF)
                nc.vector.quantize_mx(
                    out=codes[:, cols].bitcast(FP8X4),
                    scales=scales[:, cols],
                    in_=grouped[half][:].rearrange("p c j -> p (c j)"),
                )
            h_codes.append(codes)
            h_scales.append(scales)

        prod = [ps.tile([P, V], F32, name=f"prod{jt}", tag=f"y{jt}") for jt in range(TILES)]

        def multiply(g):
            for jt in range(TILES):
                nc.tensor.matmul_mx(
                    out=prod[jt][:],
                    lhsT=x_codes[(g, jt)].bitcast(FP8X4),
                    lhsT_scale=x_sc[4 * g : P, jt * P : (jt + 1) * P],
                    rhs=h_codes[g][:].bitcast(FP8X4),
                    rhs_scale=h_scales[g][:],
                    start=(g == 0),
                    stop=(g == PASSES - 1),
                )

        multiply(0)

        low = [ps.tile([P, S], F32, name=f"low{tt}", tag=f"low{tt}") for tt in range(TILES)]
        base = {}
        for half in range(2):
            for jt in range(TILES):
                base[(half, jt)] = sb.tile([P, HALF], F32, name=f"base{half}{jt}")
                nc.scalar.activation(
                    base[(half, jt)][:], q_row[:, half * HALF : (half + 1) * HALF], ACT.Identity,
                    bias=neg_r2[:, jt : jt + 1], scale=two_err[:, jt : jt + 1],
                )

        def add_into_low(half, jt, values, start, stop):
            for i in range(2):
                nc.tensor.matmul(
                    low[2 * half + i][:, jt * P : (jt + 1) * P],
                    values[:, i * P : (i + 1) * P], ident[:],
                    start=start, stop=stop, is_transpose=True,
                )

        for jt in range(TILES):
            add_into_low(0, jt, base[(0, jt)], jt == 0, False)

        for half in range(2):
            part = sb.tile([P, HALF], U32, name=f"x_codes1{half}", align_bytes=64)
            nc.vector.tensor_copy(
                part[:], x_tab[1][:].indirect(offsets[:, half * 16 : (half + 1) * 16])
            )
            for i in range(2):
                x_codes[(1, 2 * half + i)] = part[:, i * P : (i + 1) * P]

        multiply(1)

        steps = [(0, 0), (1, 0), (0, 1), (0, 2), (0, 3), (1, 1), (1, 2), (1, 3)]
        top = {}

        def finish(half):
            top_bank = ps.tile([P, 2, P], F32, name=f"top_bank{half}", tag=f"y{half}")
            for i in range(2):
                nc.tensor.matmul(
                    top_bank[:, i, :], neg_r2[:, 0:1].to_broadcast([P, P]), ident[:],
                    start=(i == 0), stop=False, is_transpose=True,
                )
            for i in range(2):
                nc.tensor.matmul(
                    top_bank[:, i, :], top[half][:, i * P : (i + 1) * P], ident[:],
                    start=False, stop=(i == 1), is_transpose=True,
                )
            best = sb.tile([P, 2], F32, name=f"best{half}")
            nc.vector.tensor_reduce(best[:], top_bank[:], AXIS.X, ALU.max, negate=True)
            for i in range(2):
                tt = 2 * half + i
                res = sb.tile([P, S], F32, name=f"res{tt}")
                if tt == TILES - 1:
                    nc.vector.tensor_scalar(
                        res[:], low[tt][:], best[:, i : i + 1], 0.0, ALU.add, ALU.max
                    )
                else:
                    nc.scalar.activation(res[:], low[tt][:], ACT.Relu, bias=best[:, i : i + 1])
                nc.sync.dma_start(out[tt * P : (tt + 1) * P, :], res[:])

        def make_term(half, jt):
            cols = slice(half * HALF, (half + 1) * HALF)
            fit = sb.tile([P, HALF], F32, name=f"fit{half}{jt}")
            nc.scalar.activation(
                fit[:], prod[jt][:, cols], ACT.Identity,
                bias=neg_err[:, jt : jt + 1], scale=slope[:, jt : jt + 1],
            )
            term = sb.tile([P, HALF], F32, name=f"term{half}{jt}")
            nc.vector.tensor_tensor(term[:], fit[:], q_row[:, cols], ALU.mult)
            add_into_low(half, jt, term, (half, jt) == (1, 0), jt == TILES - 1)
            if (half, jt) == (1, 0):
                for other in range(TILES):
                    add_into_low(1, other, base[(1, other)], False, False)
            return term

        def take_maximum(half, jt, term):
            if jt == 0:
                top[half] = term
            else:
                nxt = sb.tile([P, HALF], F32, name=f"top{half}{jt}")
                nc.vector.scalar_tensor_tensor(
                    nxt[:], term[:], shift[:, jt : jt + 1], top[half][:], ALU.add, ALU.max
                )
                top[half] = nxt
            if jt == TILES - 1:
                finish(half)

        terms = []
        for n, (half, jt) in enumerate(steps):
            terms.append(make_term(half, jt))
            if n > 0:
                take_maximum(*steps[n - 1], terms[n - 1])
        take_maximum(*steps[-1], terms[-1])
